import numpy as np
import ml_dtypes


def mxq(x, axis, fmt="e4m3"):
    dtype, down = {"e4m3": (ml_dtypes.float8_e4m3fn, 7), "e5m2": (ml_dtypes.float8_e5m2, 14)}[fmt]
    v = np.moveaxis(np.asarray(x, np.float32).astype(ml_dtypes.bfloat16).astype(np.float64), axis, -1)
    blocks = v.reshape(v.shape[:-1] + (-1, 32))
    amax = np.abs(blocks).max(-1, keepdims=True)
    byte = np.maximum(np.where(amax > 0, np.frexp(amax)[1] - 1 + 127, 0) - down, 1)
    scale = np.exp2(byte - 127.0)
    codes = (blocks / scale).astype(np.float32).astype(dtype).astype(np.float64)
    return np.moveaxis((codes * scale).reshape(v.shape), -1, axis)


WIDE = False


def mx_kscale(k):
    if not WIDE:
        return np.ones(k)
    levels = np.array([10, -10, 5, -5, 0])
    if k % 512:
        return np.exp2(np.random.permutation(np.resize(levels, k // 32))).repeat(32)
    a = np.empty((k // 512, 16))
    for p in range(k // 512):
        a[p, :8] = np.random.permutation(np.resize(levels, 8))
        for g in range(8):
            far = levels[np.abs(levels - a[p, g]) >= 10]
            a[p, g + 8] = far[np.random.randint(len(far))]
    return np.exp2(a.ravel()).repeat(32)


def f64(x):
    return np.asarray(x).astype(np.float64)


def striped(idx):
    return np.tile(idx.reshape(-1, 16).T, (8, 1)).astype(np.uint16)


def unstriped(offs):
    return offs[:16].T.reshape(-1).astype(np.int64)


def striped8(idx):
    return np.concatenate([x.reshape(-1, 16).T for x in idx]).astype(np.uint16)


def runs(offs, k):
    lists = np.stack([offs[16 * r : 16 * r + 16].T.reshape(-1) for r in range(8)]).astype(np.int64)
    return lists[np.arange(k) % 512 // 64]


def pack_weight(w):
    k, n = w.shape
    w = f64(np.asarray(w, np.float32).astype(ml_dtypes.bfloat16)).reshape(k // 32, 32, n)
    amax = np.abs(w).max(1)
    byte = np.clip(np.where(amax > 0, np.frexp(amax)[1] - 1 + 127 - 7, 1), 1, 254)
    scaled = (w * np.exp2(127.0 - byte)[:, None, :]).reshape(k, n).astype(np.float32)
    words = np.ascontiguousarray(scaled.reshape(k // 512, 128, 4, n).transpose(0, 1, 3, 2)).astype(ml_dtypes.float8_e4m3fn).view(np.uint8)
    return words, np.ascontiguousarray(byte.astype(np.uint8).reshape(k // 512, 16, n))


def unpack_weight(words, scales):
    g, p, n, _ = words.shape
    vals = np.ascontiguousarray(words).view(ml_dtypes.float8_e4m3fn).astype(np.float64) * np.repeat(np.exp2(scales.astype(np.float64) - 127.0), 8, axis=1)[..., None]
    return vals.transpose(0, 1, 3, 2).reshape(g * 512, n)


def sigmoid(v):
    return 1.0 / (1.0 + np.exp(-np.maximum(v, -700.0)))


K, T, S, G, H, U = 512, 2048, 256, 2048, 512, 512


def setup_inputs():
    n = np.random.standard_normal
    s = mx_kscale(K)[:, None]
    packed_xT = pack_weight(n((K, T)) * s)
    packed_dT = pack_weight(n((K, G)) / s)
    perm = np.random.permutation(U)
    return {
        "x_words": packed_xT[0],
        "x_scales": packed_xT[1],
        "d_words": packed_dT[0],
        "d_scales": packed_dT[1],
        "sl": np.random.uniform(1.0, 2.0, (H, 1)).astype(np.float32),
        "th": (0.5 * n((H, 1))).astype(np.float32),
        "gs": (np.random.uniform(0.5, 1.5, (K, 1)) * s).astype(np.float32),
        "offs": striped(np.random.permutation(T)[:S]),
        "ci": striped(np.random.permutation(G)[:H]),
        "n1": striped8(np.stack([np.random.permutation(S) for _ in range(8)])),
        "n2": striped8(np.stack([np.random.permutation(S) for _ in range(8)])),
        "k1": striped8(np.random.randint(0, G, (8, H))),
        "n3": striped(perm[:S]),
        "n4": striped(perm[S:]),
        "n5": striped(np.random.permutation(U)),
    }


def reference(x_words, x_scales, d_words, d_scales, sl, th, gs, offs, ci, n1, n2, k1, n3, n4, n5):
    d_k1 = unpack_weight(d_words, d_scales)[np.arange(K)[:, None], runs(k1, K)]
    d_ci = unpack_weight(d_words, d_scales)[:, unstriped(ci)]
    xq = unpack_weight(x_words, x_scales)[:, unstriped(offs)]
    s = 0.0625 * (d_ci.T @ xq)
    st = np.maximum(s, s[np.arange(H)[:, None], runs(n1, H)])
    sg = sigmoid(f64(sl) * (st[np.arange(H)[:, None], runs(n2, H)] - f64(th)))
    z = f64(gs) * (st * sg)
    h = 0.0625 * ((d_k1.T @ mxq(z, 0, "e4m3")))
    nw = 0.5 * h
    ph = np.zeros((H, U))
    ph[:, unstriped(n3)] = h
    pg = ph.copy()
    pg[:, unstriped(n4)] = nw
    return pg - pg[:, unstriped(n5)]

@@ -1,0 +1,195 @@
+from contextlib import ExitStack
+
+import concourse.mybir as mybir
+
+K, T, S, G, H, U = 512, 2048, 256, 2048, 512, 512
+FLOPS = 2 * K * H * S * 2
+
+F32 = mybir.dt.float32
+BF16 = mybir.dt.bfloat16
+I32 = mybir.dt.int32
+U32 = mybir.dt.uint32
+U16 = mybir.dt.uint16
+U8 = mybir.dt.uint8
+FP8X4 = mybir.dt.float8_e4m3fn_x4
+ALU = mybir.AluOpType
+ACT = mybir.ActivationFunctionType
+
+P = 128
+PACK = 4
+HALF = S // 2
+LEAD = 512
+
+
+def entries(lst, start, count):
+    return lst[:, start // 16 : (start + count) // 16]
+
+
+def tile_picked_dwqehhpagtwo_none_p_kernel(
+    tc, x_words, x_scales, d_words, d_scales, sl, th, gs, offs, ci, n1, n2, k1, n3, n4, n5, out
+):
+    nc = tc.nc
+    with ExitStack() as ctx:
+        keep = ctx.enter_context(tc.tile_pool(name="keep", bufs=1))
+        psum = ctx.enter_context(tc.psum_pool(name="psum", bufs=1))
+
+        def load_list(name, src):
+            tile = keep.tile(list(src.shape), U16, name=name)
+            nc.sync.dma_start(tile[:], src)
+            return tile
+
+        def load_words(tile, src, cols):
+            nc.sync.dma_start(tile[:].bitcast(I32)[:, cols], src[0].rearrange("p c r -> p (c r)").bitcast(I32)[:, cols])
+
+        def load_scale_rows(name, src, engine):
+            tile = keep.tile([P, src.shape[2]], U8, name=name)
+            engine.memset(tile[:].bitcast(I32), 0)
+            for q in range(4):
+                nc.sync.dma_start(tile[32 * q : 32 * q + 4, :].bitcast(I32), src[0, 4 * q : 4 * q + 4, :].bitcast(I32))
+            return tile
+
+        def load_row_values(name, src):
+            tile = keep.tile([P, PACK], F32, name=name)
+            nc.gpsimd.dma_start(tile[:], src.rearrange("(p t) o -> p (t o)", t=PACK))
+            return tile
+
+        d_w = keep.tile([P, G], U32, name="d_w")
+        x_w = keep.tile([P, T], U32, name="x_w")
+        load_words(d_w, d_words, slice(0, LEAD))
+        d_sc = load_scale_rows("d_sc", d_scales, nc.vector)
+        ci_l = load_list("ci_l", ci)
+        offs_l = load_list("offs_l", offs)
+        load_words(d_w, d_words, slice(LEAD, G))
+        x_sc = load_scale_rows("x_sc", x_scales, nc.vector)
+        load_words(x_w, x_words, slice(0, T))
+        n1_l = load_list("n1_l", n1)
+        k1_l = load_list("k1_l", k1)
+        d_sc8 = keep.tile([P, G], U8, name="d_sc8")
+        nc.vector.memset(d_sc8[:].bitcast(I32), 0)
+        nc.sync.dma_start(d_sc8[0:P:8, :].bitcast(I32), d_scales[0].bitcast(I32))
+        n2_l = load_list("n2_l", n2)
+        sl_t = load_row_values("sl_t", sl)
+        th_t = load_row_values("th_t", th)
+        gs_t = load_row_values("gs_t", gs)
+        n3_l = load_list("n3_l", n3)
+        n4_l = load_list("n4_l", n4)
+        n5_l = load_list("n5_l", n5)
+
+        k_sc = [keep.tile([P, 2 * P], U8, name=f"k_sc{u}", align_bytes=64) for u in range(2)]
+        for u in range(2):
+            nc.vector.memset(k_sc[u][:].bitcast(I32), 0)
+        pages = [keep.tile([P, U], F32, name=f"page{t}") for t in range(PACK)]
+
+        ci_b = keep.tile([P, H], U8, name="ci_b", tag="bytes0", align_bytes=64)
+        nc.vector.tensor_copy(ci_b[:].rearrange("p (t m) -> p m t", t=PACK), d_sc[:].indirect(ci_l[:]))
+        ci_w = keep.tile([P, H], U32, name="ci_w", tag="words0", align_bytes=64)
+        nc.vector.tensor_copy(ci_w[:].rearrange("p (t m) -> p m t", t=PACK), d_w[:].indirect(ci_l[:]))
+        x_b = keep.tile([P, S], U8, name="x_b", tag="bytes1", align_bytes=64)
+        nc.vector.tensor_copy(x_b[:], x_sc[:].indirect(offs_l[:]))
+        x_c = keep.tile([P, S], U32, name="x_c", tag="words1", align_bytes=64)
+        nc.vector.tensor_copy(x_c[:], x_w[:].indirect(offs_l[:]))
+
+        s_sb = []
+        for t in range(PACK):
+            bank = psum.tile([P, S], F32, name=f"s_ps{t}", tag=f"bank{t}")
+            cols = slice(t * P, (t + 1) * P)
+            nc.tensor.matmul_mx(
+                out=bank[:], lhsT=ci_w[:, cols].bitcast(FP8X4), lhsT_scale=ci_b[:, cols],
+                rhs=x_c[:].bitcast(FP8X4), rhs_scale=x_b[:], start=True, stop=True,
+            )
+            s_t = keep.tile([P, S], F32, name=f"s{t}")
+            nc.vector.tensor_scalar(s_t[:], bank[:], 0.0625, None, ALU.mult)
+            s_sb.append(s_t)
+
+        bias = keep.tile([P, PACK], F32, name="bias")
+        sl_th = keep.tile([P, PACK], F32, name="sl_th")
+        nc.gpsimd.tensor_tensor(sl_th[:], sl_t[:], th_t[:], ALU.mult)
+        nc.gpsimd.tensor_scalar(bias[:], sl_th[:], -1.0, None, ALU.mult)
+
+        k_w = []
+
+        def gather_k1(u):
+            part = entries(k1_l, 2 * P * u, 2 * P)
+            k_b = keep.tile([P, 2 * P], U8, name=f"k_b{u}", tag=f"bytes{u}", align_bytes=64)
+            nc.vector.tensor_copy(k_b[:], d_sc8[:].indirect(part))
+            for r in range(4):
+                nc.sync.dma_start(k_sc[u][r:P:32, :].bitcast(I32), k_b[8 * r : P : 32, :].bitcast(I32))
+            words = keep.tile([P, 2 * P], U32, name=f"k_w{u}", tag=f"words{u}", align_bytes=64)
+            nc.vector.tensor_copy(words[:], d_w[:].indirect(part))
+            k_w.append(words)
+
+        st_sb = []
+        for t in range(PACK):
+            g1 = keep.tile([P, S], F32, name=f"g1_{t}")
+            for c in (0, HALF):
+                nc.scalar.activation(g1[:, c : c + HALF], s_sb[t][:].indirect(entries(n1_l, c, HALF)), ACT.Copy)
+            st_t = keep.tile([P, S], F32, name=f"st{t}")
+            nc.vector.tensor_tensor(st_t[:], s_sb[t][:], g1[:], ALU.max)
+            st_sb.append(st_t)
+        gather_k1(0)
+
+        h_sb = [keep.tile([P, S], F32, name=f"h{t}") for t in range(PACK)]
+        z_q = []
+        for a in range(2):
+            js = slice(a * HALF, (a + 1) * HALF)
+            z_pl = keep.tile([P, PACK, HALF], BF16, name=f"z_pl{a}")
+            for t in range(PACK):
+                sg = keep.tile([P, HALF], F32, name=f"sg{a}{t}")
+                nc.scalar.activation(
+                    sg[:], st_sb[t][:].indirect(entries(n2_l, a * HALF, HALF)), ACT.Sigmoid,
+                    bias=bias[:, t : t + 1], scale=sl_t[:, t : t + 1],
+                )
+                nc.vector.scalar_tensor_tensor(z_pl[:, t, :], st_sb[t][:, js], gs_t[:, t : t + 1], sg[:], ALU.mult, ALU.mult)
+            z_il = keep.tile([P, HALF, PACK], BF16, name=f"z_il{a}", align_bytes=64)
+            nc.vector.tensor_copy(z_il[:], z_pl[:].rearrange("p t j -> p j t"))
+            z_w = keep.tile([P, HALF], U32, name=f"z_w{a}", align_bytes=64)
+            z_b = keep.tile([P, HALF], U8, name=f"z_b{a}", align_bytes=64)
+            nc.vector.quantize_mx(out=z_w[:].bitcast(FP8X4), scales=z_b[:], in_=z_il[:].rearrange("p j t -> p (j t)"))
+            z_q.append((z_w, z_b))
+
+        def second_product(t, a):
+            z_w, z_b = z_q[a]
+            bank = psum.tile([P, HALF], F32, name=f"h_ps{t}{a}", tag=f"bank{PACK * (1 - a) + t}")
+            cols = slice((t % 2) * P, (t % 2 + 1) * P)
+            nc.tensor.matmul_mx(
+                out=bank[:], lhsT=k_w[t // 2][:, cols].bitcast(FP8X4), lhsT_scale=k_sc[t // 2][:, cols],
+                rhs=z_w[:].bitcast(FP8X4), rhs_scale=z_b[:], start=True, stop=True,
+            )
+            nc.vector.tensor_scalar(h_sb[t][:, a * HALF : (a + 1) * HALF], bank[:], 0.0625, None, ALU.mult)
+
+        def scatter(t, lst, factor, start, count):
+            nc.scalar.activation(
+                pages[t][:].indirect(entries(lst, start, count)), h_sb[t][:, start : start + count], ACT.Copy, scale=factor
+            )
+
+        def finish(t, start, count):
+            ws = slice(start, start + count)
+            g5 = keep.tile([P, count], F32, name=f"g5_{t}_{start}")
+            for c in range(0, count, S):
+                n = min(S, count - c)
+                nc.scalar.activation(g5[:, c : c + n], pages[t][:].indirect(entries(n5_l, start + c, n)), ACT.Copy)
+            res = keep.tile([P, count], F32, name=f"res{t}_{start}")
+            nc.vector.tensor_tensor(res[:], pages[t][:, ws], g5[:], ALU.subtract)
+            nc.sync.dma_start(out[t * P : (t + 1) * P, ws], res[:])
+
+        for a in range(2):
+            for t in (0, 1):
+                second_product(t, a)
+        gather_k1(1)
+        for a in range(2):
+            for t in (2, 3):
+                second_product(t, a)
+        for a in range(2):
+            for lst, factor in ((n3_l, 1.0), (n4_l, 0.5)):
+                for t in (0, 1):
+                    scatter(t, lst, factor, a * HALF, HALF)
+        finish(0, 0, U)
+        scatter(2, n3_l, 1.0, 0, S)
+        finish(1, 0, U)
+        scatter(3, n3_l, 1.0, 0, S)
+        scatter(2, n4_l, 0.5, 0, S)
+        scatter(3, n4_l, 0.5, 0, S)
+        finish(2, 0, U)
+        finish(3, 0, 256)
+        finish(3, 256, 128)
+        finish(3, 384, 128)

@@ -53,6 +53,10 @@ def tile_picked_dwqehhpagtwo_none_p_kernel(
             nc.gpsimd.dma_start(tile[:], src.rearrange("(p t) o -> p (t o)", t=PACK))
             return tile
 
+        warm = keep.tile([P, 16], F32, name="warm")
+        nc.gpsimd.memset(warm[:, 0:1], 0.0)
+        nc.scalar.activation(warm[:, 8:9], warm[:, 0:1], ACT.Sigmoid)
+
         d_w = keep.tile([P, G], U32, name="d_w")
         x_w = keep.tile([P, T], U32, name="x_w")
         load_words(d_w, d_words, slice(0, LEAD))

@@ -18,7 +18,9 @@ ACT = mybir.ActivationFunctionType
 P = 128
 PACK = 4
 HALF = S // 2
-LEAD = 512
+LEAD = 1024
+PAGE = U + 32
+X_ROW = 4
 
 
 def entries(lst, start, count):
@@ -41,11 +43,11 @@ def tile_picked_dwqehhpagtwo_none_p_kernel(
         def load_words(tile, src, cols):
             nc.sync.dma_start(tile[:].bitcast(I32)[:, cols], src[0].rearrange("p c r -> p (c r)").bitcast(I32)[:, cols])
 
-        def load_scale_rows(name, src, engine):
+        def load_scale_rows(name, src, row):
             tile = keep.tile([P, src.shape[2]], U8, name=name)
-            engine.memset(tile[:].bitcast(I32), 0)
+            nc.vector.memset(tile[:].bitcast(I32), 0)
             for q in range(4):
-                nc.sync.dma_start(tile[32 * q : 32 * q + 4, :].bitcast(I32), src[0, 4 * q : 4 * q + 4, :].bitcast(I32))
+                nc.sync.dma_start(tile[32 * q + row : 32 * q + row + 4, :].bitcast(I32), src[0, 4 * q : 4 * q + 4, :].bitcast(I32))
             return tile
 
         def load_row_values(name, src):
@@ -58,19 +60,20 @@ def tile_picked_dwqehhpagtwo_none_p_kernel(
         nc.scalar.activation(warm[:, 8:9], warm[:, 0:1], ACT.Sigmoid)
 
         d_w = keep.tile([P, G], U32, name="d_w")
-        x_w = keep.tile([P, T], U32, name="x_w")
+        x_w = keep.tile([P, T], U32, name="x_w", tag="x_w", align_bytes=64)
         load_words(d_w, d_words, slice(0, LEAD))
-        d_sc = load_scale_rows("d_sc", d_scales, nc.vector)
+        d_sc = load_scale_rows("d_sc", d_scales, 0)
         ci_l = load_list("ci_l", ci)
-        offs_l = load_list("offs_l", offs)
         load_words(d_w, d_words, slice(LEAD, G))
-        x_sc = load_scale_rows("x_sc", x_scales, nc.vector)
-        load_words(x_w, x_words, slice(0, T))
-        n1_l = load_list("n1_l", n1)
-        k1_l = load_list("k1_l", k1)
+        load_words(x_w, x_words, slice(0, LEAD))
+        offs_l = load_list("offs_l", offs)
+        x_sc = load_scale_rows("x_sc", x_scales, X_ROW)
+        load_words(x_w, x_words, slice(LEAD, T))
         d_sc8 = keep.tile([P, G], U8, name="d_sc8")
         nc.vector.memset(d_sc8[:].bitcast(I32), 0)
-        nc.sync.dma_start(d_sc8[0:P:8, :].bitcast(I32), d_scales[0].bitcast(I32))
+        nc.gpsimd.dma_start(d_sc8[0:P:8, :].bitcast(I32), d_scales[0].bitcast(I32))
+        k1_l = load_list("k1_l", k1)
+        n1_l = load_list("n1_l", n1)
         n2_l = load_list("n2_l", n2)
         sl_t = load_row_values("sl_t", sl)
         th_t = load_row_values("th_t", th)
@@ -82,71 +85,74 @@ def tile_picked_dwqehhpagtwo_none_p_kernel(
         k_sc = [keep.tile([P, 2 * P], U8, name=f"k_sc{u}", align_bytes=64) for u in range(2)]
         for u in range(2):
             nc.vector.memset(k_sc[u][:].bitcast(I32), 0)
-        pages = [keep.tile([P, U], F32, name=f"page{t}") for t in range(PACK)]
+        pages = [keep.tile([P, PAGE], F32, name=f"page{t}") for t in range(PACK)]
+        s_sb = [keep.tile([P, 2 * S], F32, name=f"s{t}") for t in range(PACK)]
+        for t in range(PACK):
+            nc.vector.memset(s_sb[t][:, S:], 0.0)
+            nc.vector.memset(pages[t][:, U:], 0.0)
 
-        ci_b = keep.tile([P, H], U8, name="ci_b", tag="bytes0", align_bytes=64)
+        ci_b = keep.tile([P, H], U8, name="ci_b", align_bytes=64)
         nc.vector.tensor_copy(ci_b[:].rearrange("p (t m) -> p m t", t=PACK), d_sc[:].indirect(ci_l[:]))
         ci_w = keep.tile([P, H], U32, name="ci_w", tag="words0", align_bytes=64)
         nc.vector.tensor_copy(ci_w[:].rearrange("p (t m) -> p m t", t=PACK), d_w[:].indirect(ci_l[:]))
-        x_b = keep.tile([P, S], U8, name="x_b", tag="bytes1", align_bytes=64)
+        x_b = keep.tile([P, S], U8, name="x_b", align_bytes=64)
         nc.vector.tensor_copy(x_b[:], x_sc[:].indirect(offs_l[:]))
-        x_c = keep.tile([P, S], U32, name="x_c", tag="words1", align_bytes=64)
+        x_c = keep.tile([P, S], U32, name="x_c", align_bytes=64)
         nc.vector.tensor_copy(x_c[:], x_w[:].indirect(offs_l[:]))
 
-        s_sb = []
         for t in range(PACK):
             bank = psum.tile([P, S], F32, name=f"s_ps{t}", tag=f"bank{t}")
             cols = slice(t * P, (t + 1) * P)
             nc.tensor.matmul_mx(
                 out=bank[:], lhsT=ci_w[:, cols].bitcast(FP8X4), lhsT_scale=ci_b[:, cols],
-                rhs=x_c[:].bitcast(FP8X4), rhs_scale=x_b[:], start=True, stop=True,
+                rhs=x_c[:].bitcast(FP8X4), rhs_scale=x_b[X_ROW:P, :], start=True, stop=True,
             )
-            s_t = keep.tile([P, S], F32, name=f"s{t}")
-            nc.vector.tensor_scalar(s_t[:], bank[:], 0.0625, None, ALU.mult)
-            s_sb.append(s_t)
+            if t == 0:
+                nc.scalar.activation(s_sb[t][:, :S], bank[:], ACT.Copy, scale=0.0625)
+            else:
+                nc.vector.tensor_scalar(s_sb[t][:, :S], bank[:], 0.0625, None, ALU.mult)
 
         bias = keep.tile([P, PACK], F32, name="bias")
         sl_th = keep.tile([P, PACK], F32, name="sl_th")
         nc.gpsimd.tensor_tensor(sl_th[:], sl_t[:], th_t[:], ALU.mult)
         nc.gpsimd.tensor_scalar(bias[:], sl_th[:], -1.0, None, ALU.mult)
 
-        k_w = []
-
-        def gather_k1(u):
-            part = entries(k1_l, 2 * P * u, 2 * P)
-            k_b = keep.tile([P, 2 * P], U8, name=f"k_b{u}", tag=f"bytes{u}", align_bytes=64)
-            nc.vector.tensor_copy(k_b[:], d_sc8[:].indirect(part))
+        def gather_k1_bytes(u, tag):
+            k_b = keep.tile([P, 2 * P], U8, name=f"k_b{u}", tag=tag, align_bytes=64)
+            nc.vector.tensor_copy(k_b[:], d_sc8[:].indirect(entries(k1_l, 2 * P * u, 2 * P)))
             for r in range(4):
                 nc.sync.dma_start(k_sc[u][r:P:32, :].bitcast(I32), k_b[8 * r : P : 32, :].bitcast(I32))
-            words = keep.tile([P, 2 * P], U32, name=f"k_w{u}", tag=f"words{u}", align_bytes=64)
-            nc.vector.tensor_copy(words[:], d_w[:].indirect(part))
-            k_w.append(words)
 
+        def gather_k1_words(u, tag):
+            words = keep.tile([P, 2 * P], U32, name=f"k_w{u}", tag=tag, align_bytes=64)
+            nc.vector.tensor_copy(words[:], d_w[:].indirect(entries(k1_l, 2 * P * u, 2 * P)))
+            return words
+
+        gather_k1_bytes(0, "x_w")
         st_sb = []
         for t in range(PACK):
-            g1 = keep.tile([P, S], F32, name=f"g1_{t}")
-            for c in (0, HALF):
-                nc.scalar.activation(g1[:, c : c + HALF], s_sb[t][:].indirect(entries(n1_l, c, HALF)), ACT.Copy)
+            g1 = keep.tile([P, S], F32, name=f"g1_{t}", tag=f"g1_{t}")
+            nc.scalar.activation(g1[:], s_sb[t][:].indirect(n1_l[:]), ACT.Copy)
             st_t = keep.tile([P, S], F32, name=f"st{t}")
-            nc.vector.tensor_tensor(st_t[:], s_sb[t][:], g1[:], ALU.max)
+            nc.vector.tensor_tensor(st_t[:], s_sb[t][:, :S], g1[:], ALU.max)
             st_sb.append(st_t)
-        gather_k1(0)
+        k_w = [gather_k1_words(0, "words0")]
 
         h_sb = [keep.tile([P, S], F32, name=f"h{t}") for t in range(PACK)]
         z_q = []
         for a in range(2):
             js = slice(a * HALF, (a + 1) * HALF)
-            z_pl = keep.tile([P, PACK, HALF], BF16, name=f"z_pl{a}")
+            z_pl = keep.tile([P, PACK, HALF], BF16, name=f"z_pl{a}", tag=f"z{a}", align_bytes=64)
+            sg = keep.tile([P, PACK, HALF], F32, name=f"sg{a}", tag=("sg0", "g1_3")[a])
             for t in range(PACK):
-                sg = keep.tile([P, HALF], F32, name=f"sg{a}{t}")
                 nc.scalar.activation(
-                    sg[:], st_sb[t][:].indirect(entries(n2_l, a * HALF, HALF)), ACT.Sigmoid,
+                    sg[:, t, :], st_sb[t][:].indirect(entries(n2_l, a * HALF, HALF)), ACT.Sigmoid,
                     bias=bias[:, t : t + 1], scale=sl_t[:, t : t + 1],
                 )
-                nc.vector.scalar_tensor_tensor(z_pl[:, t, :], st_sb[t][:, js], gs_t[:, t : t + 1], sg[:], ALU.mult, ALU.mult)
-            z_il = keep.tile([P, HALF, PACK], BF16, name=f"z_il{a}", align_bytes=64)
+                nc.vector.scalar_tensor_tensor(z_pl[:, t, :], st_sb[t][:, js], gs_t[:, t : t + 1], sg[:, t, :], ALU.mult, ALU.mult)
+            z_il = keep.tile([P, HALF, PACK], BF16, name=f"z_il{a}", tag=f"z{a + 1}", align_bytes=64)
             nc.vector.tensor_copy(z_il[:], z_pl[:].rearrange("p t j -> p j t"))
-            z_w = keep.tile([P, HALF], U32, name=f"z_w{a}", align_bytes=64)
+            z_w = keep.tile([P, HALF], U32, name=f"z_w{a}", tag=f"z_w{a}", align_bytes=64)
             z_b = keep.tile([P, HALF], U8, name=f"z_b{a}", align_bytes=64)
             nc.vector.quantize_mx(out=z_w[:].bitcast(FP8X4), scales=z_b[:], in_=z_il[:].rearrange("p j t -> p (j t)"))
             z_q.append((z_w, z_b))
@@ -159,27 +165,30 @@ def tile_picked_dwqehhpagtwo_none_p_kernel(
                 out=bank[:], lhsT=k_w[t // 2][:, cols].bitcast(FP8X4), lhsT_scale=k_sc[t // 2][:, cols],
                 rhs=z_w[:].bitcast(FP8X4), rhs_scale=z_b[:], start=True, stop=True,
             )
-            nc.vector.tensor_scalar(h_sb[t][:, a * HALF : (a + 1) * HALF], bank[:], 0.0625, None, ALU.mult)
+            dst = h_sb[t][:, a * HALF : (a + 1) * HALF]
+            if t < 2 and a == 0:
+                nc.scalar.activation(dst, bank[:], ACT.Copy, scale=0.0625)
+            else:
+                nc.vector.tensor_scalar(dst, bank[:], 0.0625, None, ALU.mult)
 
         def scatter(t, lst, factor, start, count):
             nc.scalar.activation(
                 pages[t][:].indirect(entries(lst, start, count)), h_sb[t][:, start : start + count], ACT.Copy, scale=factor
             )
 
-        def finish(t, start, count):
+        def finish(t, start, count, tag):
             ws = slice(start, start + count)
             g5 = keep.tile([P, count], F32, name=f"g5_{t}_{start}")
-            for c in range(0, count, S):
-                n = min(S, count - c)
-                nc.scalar.activation(g5[:, c : c + n], pages[t][:].indirect(entries(n5_l, start + c, n)), ACT.Copy)
-            res = keep.tile([P, count], F32, name=f"res{t}_{start}")
+            nc.scalar.activation(g5[:], pages[t][:].indirect(entries(n5_l, start, count)), ACT.Copy)
+            res = keep.tile([P, count], F32, name=f"res{t}_{start}", tag=tag, align_bytes=64)
             nc.vector.tensor_tensor(res[:], pages[t][:, ws], g5[:], ALU.subtract)
             nc.sync.dma_start(out[t * P : (t + 1) * P, ws], res[:])
 
         for a in range(2):
             for t in (0, 1):
                 second_product(t, a)
-        gather_k1(1)
+        gather_k1_bytes(1, "z1")
+        k_w.append(gather_k1_words(1, "z2"))
         for a in range(2):
             for t in (2, 3):
                 second_product(t, a)
@@ -187,13 +196,12 @@ def tile_picked_dwqehhpagtwo_none_p_kernel(
             for lst, factor in ((n3_l, 1.0), (n4_l, 0.5)):
                 for t in (0, 1):
                     scatter(t, lst, factor, a * HALF, HALF)
-        finish(0, 0, U)
+        finish(0, 0, U, "z2")
         scatter(2, n3_l, 1.0, 0, S)
-        finish(1, 0, U)
+        finish(1, 0, U, "z_w1")
         scatter(3, n3_l, 1.0, 0, S)
         scatter(2, n4_l, 0.5, 0, S)
         scatter(3, n4_l, 0.5, 0, S)
-        finish(2, 0, U)
-        finish(3, 0, 256)
-        finish(3, 256, 128)
-        finish(3, 384, 128)
+        finish(2, 0, U, "res2")
+        finish(3, 0, 384, "res3")
+        finish(3, 384, 128, "res4")

@@ -98,19 +98,26 @@ def tile_picked_dwqehhpagtwo_none_p_kernel(
         x_b = keep.tile([P, S], U8, name="x_b", align_bytes=64)
         nc.vector.tensor_copy(x_b[:], x_sc[:].indirect(offs_l[:]))
         x_c = keep.tile([P, S], U32, name="x_c", align_bytes=64)
-        nc.vector.tensor_copy(x_c[:], x_w[:].indirect(offs_l[:]))
+        for c in (0, HALF):
+            nc.vector.tensor_copy(x_c[:, c : c + HALF], x_w[:].indirect(entries(offs_l, c, HALF)))
 
-        for t in range(PACK):
-            bank = psum.tile([P, S], F32, name=f"s_ps{t}", tag=f"bank{t}")
+        def first_product(t, start, count, tag):
+            bank = psum.tile([P, count], F32, name=f"s_ps{t}_{start}", tag=tag)
             cols = slice(t * P, (t + 1) * P)
+            js = slice(start, start + count)
             nc.tensor.matmul_mx(
                 out=bank[:], lhsT=ci_w[:, cols].bitcast(FP8X4), lhsT_scale=ci_b[:, cols],
-                rhs=x_c[:].bitcast(FP8X4), rhs_scale=x_b[X_ROW:P, :], start=True, stop=True,
+                rhs=x_c[:, js].bitcast(FP8X4), rhs_scale=x_b[X_ROW:P, js], start=True, stop=True,
             )
             if t == 0:
-                nc.scalar.activation(s_sb[t][:, :S], bank[:], ACT.Copy, scale=0.0625)
+                nc.scalar.activation(s_sb[t][:, js], bank[:], ACT.Copy, scale=0.0625)
             else:
-                nc.vector.tensor_scalar(s_sb[t][:, :S], bank[:], 0.0625, None, ALU.mult)
+                nc.vector.tensor_scalar(s_sb[t][:, js], bank[:], 0.0625, None, ALU.mult)
+
+        first_product(0, 0, HALF, "bank4")
+        first_product(0, HALF, HALF, "bank0")
+        for t in range(1, PACK):
+            first_product(t, 0, S, f"bank{t}")
 
         bias = keep.tile([P, PACK], F32, name="bias")
         sl_th = keep.tile([P, PACK], F32, name="sl_th")
@@ -203,5 +210,6 @@ def tile_picked_dwqehhpagtwo_none_p_kernel(
         scatter(2, n4_l, 0.5, 0, S)
         scatter(3, n4_l, 0.5, 0, S)
         finish(2, 0, U, "res2")
-        finish(3, 0, 384, "res3")
-        finish(3, 384, 128, "res4")
+        finish(3, 0, 256, "res3")
+        finish(3, 256, 128, "res4")
+        finish(3, 384, 128, "res5")

@@ -52,7 +52,7 @@ def tile_picked_dwqehhpagtwo_none_p_kernel(
 
         def load_row_values(name, src):
             tile = keep.tile([P, PACK], F32, name=name)
-            nc.gpsimd.dma_start(tile[:], src.rearrange("(p t) o -> p (t o)", t=PACK))
+            nc.sync.dma_start(tile[:], src.rearrange("(p t) o -> p (t o)", t=PACK))
             return tile
 
         warm = keep.tile([P, 16], F32, name="warm")
@@ -71,12 +71,12 @@ def tile_picked_dwqehhpagtwo_none_p_kernel(
         load_words(x_w, x_words, slice(LEAD, T))
         d_sc8 = keep.tile([P, G], U8, name="d_sc8")
         nc.vector.memset(d_sc8[:].bitcast(I32), 0)
-        nc.gpsimd.dma_start(d_sc8[0:P:8, :].bitcast(I32), d_scales[0].bitcast(I32))
+        nc.sync.dma_start(d_sc8[0:P:8, :].bitcast(I32), d_scales[0].bitcast(I32))
         k1_l = load_list("k1_l", k1)
         n1_l = load_list("n1_l", n1)
-        n2_l = load_list("n2_l", n2)
         sl_t = load_row_values("sl_t", sl)
         th_t = load_row_values("th_t", th)
+        n2_l = load_list("n2_l", n2)
         gs_t = load_row_values("gs_t", gs)
         n3_l = load_list("n3_l", n3)
         n4_l = load_list("n4_l", n4)

from contextlib import ExitStack

import concourse.mybir as mybir

K, T, S, G, H, U = 512, 2048, 256, 2048, 512, 512
FLOPS = 2 * K * H * S * 2

F32 = mybir.dt.float32
BF16 = mybir.dt.bfloat16
I32 = mybir.dt.int32
U32 = mybir.dt.uint32
U16 = mybir.dt.uint16
U8 = mybir.dt.uint8
FP8X4 = mybir.dt.float8_e4m3fn_x4
ALU = mybir.AluOpType
ACT = mybir.ActivationFunctionType

P = 128
PACK = 4
HALF = S // 2
LEAD = 1024
PAGE = U + 32
X_ROW = 4


def entries(lst, start, count):
    return lst[:, start // 16 : (start + count) // 16]


def tile_picked_dwqehhpagtwo_none_p_kernel(
    tc, x_words, x_scales, d_words, d_scales, sl, th, gs, offs, ci, n1, n2, k1, n3, n4, n5, out
):
    nc = tc.nc
    with ExitStack() as ctx:
        keep = ctx.enter_context(tc.tile_pool(name="keep", bufs=1))
        psum = ctx.enter_context(tc.psum_pool(name="psum", bufs=1))

        def load_list(name, src):
            tile = keep.tile(list(src.shape), U16, name=name)
            nc.sync.dma_start(tile[:], src)
            return tile

        def load_words(tile, src, cols):
            nc.sync.dma_start(tile[:].bitcast(I32)[:, cols], src[0].rearrange("p c r -> p (c r)").bitcast(I32)[:, cols])

        def load_scale_rows(name, src, row):
            tile = keep.tile([P, src.shape[2]], U8, name=name)
            nc.vector.memset(tile[:].bitcast(I32), 0)
            for q in range(4):
                nc.sync.dma_start(tile[32 * q + row : 32 * q + row + 4, :].bitcast(I32), src[0, 4 * q : 4 * q + 4, :].bitcast(I32))
            return tile

        def load_row_values(name, src):
            tile = keep.tile([P, PACK], F32, name=name)
            nc.sync.dma_start(tile[:], src.rearrange("(p t) o -> p (t o)", t=PACK))
            return tile

        warm = keep.tile([P, 16], F32, name="warm")
        nc.gpsimd.memset(warm[:, 0:1], 0.0)
        nc.scalar.activation(warm[:, 8:9], warm[:, 0:1], ACT.Sigmoid)

        d_w = keep.tile([P, G], U32, name="d_w")
        x_w = keep.tile([P, T], U32, name="x_w", tag="x_w", align_bytes=64)
        load_words(d_w, d_words, slice(0, LEAD))
        d_sc = load_scale_rows("d_sc", d_scales, 0)
        ci_l = load_list("ci_l", ci)
        load_words(d_w, d_words, slice(LEAD, G))
        load_words(x_w, x_words, slice(0, LEAD))
        offs_l = load_list("offs_l", offs)
        x_sc = load_scale_rows("x_sc", x_scales, X_ROW)
        load_words(x_w, x_words, slice(LEAD, T))
        d_sc8 = keep.tile([P, G], U8, name="d_sc8")
        nc.vector.memset(d_sc8[:].bitcast(I32), 0)
        nc.sync.dma_start(d_sc8[0:P:8, :].bitcast(I32), d_scales[0].bitcast(I32))
        k1_l = load_list("k1_l", k1)
        n1_l = load_list("n1_l", n1)
        sl_t = load_row_values("sl_t", sl)
        th_t = load_row_values("th_t", th)
        n2_l = load_list("n2_l", n2)
        gs_t = load_row_values("gs_t", gs)
        n3_l = load_list("n3_l", n3)
        n4_l = load_list("n4_l", n4)
        n5_l = load_list("n5_l", n5)

        k_sc = [keep.tile([P, 2 * P], U8, name=f"k_sc{u}", align_bytes=64) for u in range(2)]
        for u in range(2):
            nc.vector.memset(k_sc[u][:].bitcast(I32), 0)
        pages = [keep.tile([P, PAGE], F32, name=f"page{t}") for t in range(PACK)]
        s_sb = [keep.tile([P, 2 * S], F32, name=f"s{t}") for t in range(PACK)]
        for t in range(PACK):
            nc.vector.memset(s_sb[t][:, S:], 0.0)
            nc.vector.memset(pages[t][:, U:], 0.0)

        ci_b = keep.tile([P, H], U8, name="ci_b", align_bytes=64)
        nc.vector.tensor_copy(ci_b[:].rearrange("p (t m) -> p m t", t=PACK), d_sc[:].indirect(ci_l[:]))
        ci_w = keep.tile([P, H], U32, name="ci_w", tag="words0", align_bytes=64)
        nc.vector.tensor_copy(ci_w[:].rearrange("p (t m) -> p m t", t=PACK), d_w[:].indirect(ci_l[:]))
        x_b = keep.tile([P, S], U8, name="x_b", align_bytes=64)
        nc.vector.tensor_copy(x_b[:], x_sc[:].indirect(offs_l[:]))
        x_c = keep.tile([P, S], U32, name="x_c", align_bytes=64)
        for c in (0, HALF):
            nc.vector.tensor_copy(x_c[:, c : c + HALF], x_w[:].indirect(entries(offs_l, c, HALF)))

        def first_product(t, start, count, tag):
            bank = psum.tile([P, count], F32, name=f"s_ps{t}_{start}", tag=tag)
            cols = slice(t * P, (t + 1) * P)
            js = slice(start, start + count)
            nc.tensor.matmul_mx(
                out=bank[:], lhsT=ci_w[:, cols].bitcast(FP8X4), lhsT_scale=ci_b[:, cols],
                rhs=x_c[:, js].bitcast(FP8X4), rhs_scale=x_b[X_ROW:P, js], start=True, stop=True,
            )
            if t == 0:
                nc.scalar.activation(s_sb[t][:, js], bank[:], ACT.Copy, scale=0.0625)
            else:
                nc.vector.tensor_scalar(s_sb[t][:, js], bank[:], 0.0625, None, ALU.mult)

        first_product(0, 0, HALF, "bank4")
        first_product(0, HALF, HALF, "bank0")
        for t in range(1, PACK):
            first_product(t, 0, S, f"bank{t}")

        bias = keep.tile([P, PACK], F32, name="bias")
        sl_th = keep.tile([P, PACK], F32, name="sl_th")
        nc.gpsimd.tensor_tensor(sl_th[:], sl_t[:], th_t[:], ALU.mult)
        nc.gpsimd.tensor_scalar(bias[:], sl_th[:], -1.0, None, ALU.mult)

        def gather_k1_bytes(u, tag):
            k_b = keep.tile([P, 2 * P], U8, name=f"k_b{u}", tag=tag, align_bytes=64)
            nc.vector.tensor_copy(k_b[:], d_sc8[:].indirect(entries(k1_l, 2 * P * u, 2 * P)))
            for r in range(4):
                nc.sync.dma_start(k_sc[u][r:P:32, :].bitcast(I32), k_b[8 * r : P : 32, :].bitcast(I32))

        def gather_k1_words(u, tag):
            words = keep.tile([P, 2 * P], U32, name=f"k_w{u}", tag=tag, align_bytes=64)
            nc.vector.tensor_copy(words[:], d_w[:].indirect(entries(k1_l, 2 * P * u, 2 * P)))
            return words

        gather_k1_bytes(0, "x_w")
        st_sb = []
        for t in range(PACK):
            g1 = keep.tile([P, S], F32, name=f"g1_{t}", tag=f"g1_{t}")
            nc.scalar.activation(g1[:], s_sb[t][:].indirect(n1_l[:]), ACT.Copy)
            st_t = keep.tile([P, S], F32, name=f"st{t}")
            nc.vector.tensor_tensor(st_t[:], s_sb[t][:, :S], g1[:], ALU.max)
            st_sb.append(st_t)
        k_w = [gather_k1_words(0, "words0")]

        h_sb = [keep.tile([P, S], F32, name=f"h{t}") for t in range(PACK)]
        z_q = []
        for a in range(2):
            js = slice(a * HALF, (a + 1) * HALF)
            z_pl = keep.tile([P, PACK, HALF], BF16, name=f"z_pl{a}", tag=f"z{a}", align_bytes=64)
            sg = keep.tile([P, PACK, HALF], F32, name=f"sg{a}", tag=("sg0", "g1_3")[a])
            for t in range(PACK):
                nc.scalar.activation(
                    sg[:, t, :], st_sb[t][:].indirect(entries(n2_l, a * HALF, HALF)), ACT.Sigmoid,
                    bias=bias[:, t : t + 1], scale=sl_t[:, t : t + 1],
                )
                nc.vector.scalar_tensor_tensor(z_pl[:, t, :], st_sb[t][:, js], gs_t[:, t : t + 1], sg[:, t, :], ALU.mult, ALU.mult)
            z_il = keep.tile([P, HALF, PACK], BF16, name=f"z_il{a}", tag=f"z{a + 1}", align_bytes=64)
            nc.vector.tensor_copy(z_il[:], z_pl[:].rearrange("p t j -> p j t"))
            z_w = keep.tile([P, HALF], U32, name=f"z_w{a}", tag=f"z_w{a}", align_bytes=64)
            z_b = keep.tile([P, HALF], U8, name=f"z_b{a}", align_bytes=64)
            nc.vector.quantize_mx(out=z_w[:].bitcast(FP8X4), scales=z_b[:], in_=z_il[:].rearrange("p j t -> p (j t)"))
            z_q.append((z_w, z_b))

        def second_product(t, a):
            z_w, z_b = z_q[a]
            bank = psum.tile([P, HALF], F32, name=f"h_ps{t}{a}", tag=f"bank{PACK * (1 - a) + t}")
            cols = slice((t % 2) * P, (t % 2 + 1) * P)
            nc.tensor.matmul_mx(
                out=bank[:], lhsT=k_w[t // 2][:, cols].bitcast(FP8X4), lhsT_scale=k_sc[t // 2][:, cols],
                rhs=z_w[:].bitcast(FP8X4), rhs_scale=z_b[:], start=True, stop=True,
            )
            dst = h_sb[t][:, a * HALF : (a + 1) * HALF]
            if t < 2 and a == 0:
                nc.scalar.activation(dst, bank[:], ACT.Copy, scale=0.0625)
            else:
                nc.vector.tensor_scalar(dst, bank[:], 0.0625, None, ALU.mult)

        def scatter(t, lst, factor, start, count):
            nc.scalar.activation(
                pages[t][:].indirect(entries(lst, start, count)), h_sb[t][:, start : start + count], ACT.Copy, scale=factor
            )

        def finish(t, start, count, tag):
            ws = slice(start, start + count)
            g5 = keep.tile([P, count], F32, name=f"g5_{t}_{start}")
            nc.scalar.activation(g5[:], pages[t][:].indirect(entries(n5_l, start, count)), ACT.Copy)
            res = keep.tile([P, count], F32, name=f"res{t}_{start}", tag=tag, align_bytes=64)
            nc.vector.tensor_tensor(res[:], pages[t][:, ws], g5[:], ALU.subtract)
            nc.sync.dma_start(out[t * P : (t + 1) * P, ws], res[:])

        for a in range(2):
            for t in (0, 1):
                second_product(t, a)
        gather_k1_bytes(1, "z1")
        k_w.append(gather_k1_words(1, "z2"))
        for a in range(2):
            for t in (2, 3):
                second_product(t, a)
        for a in range(2):
            for lst, factor in ((n3_l, 1.0), (n4_l, 0.5)):
                for t in (0, 1):
                    scatter(t, lst, factor, a * HALF, HALF)
        finish(0, 0, U, "z2")
        scatter(2, n3_l, 1.0, 0, S)
        finish(1, 0, U, "z_w1")
        scatter(3, n3_l, 1.0, 0, S)
        scatter(2, n4_l, 0.5, 0, S)
        scatter(3, n4_l, 0.5, 0, S)
        finish(2, 0, U, "res2")
        finish(3, 0, 256, "res3")
        finish(3, 256, 128, "res4")
        finish(3, 384, 128, "res5")
